import numpy as np, ml_dtypes
CORES = [24,26,29,31,48,50,53,55]
N = 8
import mx_ref
NC, G = 256, 4
C = np.float32(0.023)
BF = ml_dtypes.bfloat16
def cut(t, i, w=512):
    return t[:, w * i:w * i + w]
def tile(rs):
    return np.stack(rs, axis=2).reshape(128, -1).astype(BF)
def layer(w, X):
    out = []
    for i in range(G):
        for t in range(len(X)):
            p = mx_ref.matmul(mx_ref.quantize(cut(w, len(X) * i + t)), X[t])
            z = p if t == 0 else z + p
        out.append(z)
    return out
def act(Z):
    return [np.maximum(z, 0) * C for z in Z]
def turned(R):
    return [np.concatenate([R[b][:, 128 * t:128 * t + 128].T for b in range(4)], axis=1) for t in range(4)]
def setup_inputs(rng):
    def f(*shape):
        return mx_ref.flush((rng.standard_normal(shape, dtype=np.float32) * np.exp2(rng.integers(-2, 3, shape[:-1] + (1,)))).astype(BF))
    return {"x": f(N, 128, 4 * 512), "w1": f(N, 128, G * 512), "w2": f(N, 128, 512), "e": f(N, 128, 4 * NC)}
def setup_inputs_blocks(rng):
    d = setup_inputs(rng)
    for k in ("x", "w1", "w2", "e"): d[k] = mx_ref.spread(d[k], rng, 4)
    return d
def setup_inputs_wide(rng):
    d = setup_inputs(rng)
    for k in ("x", "w1", "w2", "e"): d[k] = mx_ref.flush((d[k].astype(np.float32) * np.exp2(rng.integers(-6, 7, (N, 1, 1))).astype(np.float32)).astype(BF))
    return d
def setup_inputs_zeros(rng):
    d = setup_inputs(rng); v = d["x"].reshape(N, 128, -1, 4).copy()
    v[np.broadcast_to((rng.random((N, 1, v.shape[2], 1)) < 0.33), v.shape)] = 0
    d["x"] = v.reshape(d["x"].shape)
    return d
def reference(x, w1, w2, e):
    R = [act(layer(w1[j], [mx_ref.quantize(x[j])])) for j in range(N)]
    H = [mx_ref.quantize(tile(R[j])) for j in range(N)]
    K = [tile(turned(R[j])) for j in range(N)]
    y = np.zeros((N, 128, 512), np.float32); z = np.zeros((N, 128, 4 * NC), np.float32)
    for r in range(N):
        y[r] = mx_ref.matmul(mx_ref.quantize(w2[r]), H[(r - 1) % N]); qe = mx_ref.quantize(e[r])
        for b in range(4):
            z[r][:, NC * b:NC * b + NC] = mx_ref.matmul(mx_ref.quantize(cut(K[(r + 1) % N], b)), qe)
    return {"y": y, "z": z}

from concourse.bass import DstId, RemoteDMATransfer
from concourse.mybir import dt, AluOpType, ActivationFunctionType

MX = "float8_e4m3fn_x4"
SCRATCH = {
    "xt": ("sbuf", [128, 2048], "bfloat16"), "wt": ("sbuf", [128, 2048], "bfloat16"),
    "vt": ("sbuf", [128, 512], "bfloat16"), "et": ("sbuf", [128, 1024], "bfloat16"),
    "ht": ("sbuf", [128, 2048], "bfloat16"), "kt": ("sbuf", [128, 2048], "bfloat16"),
    "qx": ("sbuf", [128, 512], MX), "sx": ("sbuf", [128, 512], "uint8"),
    "qw": ("sbuf", [128, 512], MX), "sw": ("sbuf", [128, 512], "uint8"),
    "qv": ("sbuf", [128, 128], MX), "sv": ("sbuf", [128, 128], "uint8"),
    "qe": ("sbuf", [128, 256], MX), "se": ("sbuf", [128, 256], "uint8"),
    "qh": ("sbuf", [128, 512], MX), "sh": ("sbuf", [128, 512], "uint8"),
    "qk": ("sbuf", [128, 512], MX), "sk": ("sbuf", [128, 512], "uint8"),
    "rqh": ("sbuf", [128, 512], MX), "rsh": ("sbuf", [128, 512], "uint8"),
    "rqk": ("sbuf", [128, 512], MX), "rsk": ("sbuf", [128, 512], "uint8"),
    "yo": ("sbuf", [128, 512], "float32"), "zo": ("sbuf", [128, 1024], "float32"),
    "pa": ("psum", [128, 2048], "float32"), "pb": ("psum", [128, 2048], "float32"),
}
SEMAPHORES = (
    ["la0", "la1", "lb0", "lb1", "lb2", "lb3", "le", "lv"]
    + ["va", "vb0", "vb1", "vb2", "vb3", "vp0", "vp1", "vp2", "vp3", "vs", "vv", "ve"]
    + ["m%d" % i for i in range(16)] + ["n%d" % i for i in range(4)]
    + ["ap0", "ap1", "ap2", "ap3", "as"]
    + ["my0", "my1", "mz0", "mz1", "mz2", "mz3", "cy0", "cy1", "cz0", "cz1", "cz2", "cz3", "sty", "stz"]
    + ["f%d" % i for i in range(10)]
    + ["ah0", "ah1", "ak0", "ak1", "sent"]
)
COEF = 0.023
RANKS = 8
ON, OFF, RA, RB, ROFF = 16, 8, 4, 8, 8
CHUNKS = [(0, 128), (128, 256), (256, 512)]
ORDER = ["b0", "b1", "p0", "b2", "p1", "p2"]
VFIRST, VSECOND = (1, 3), (1, 3)
WHOLE = [("q", 0, 128, 0, 0), ("q", 128, 512, 2, 0), ("s", 0, 512, 2, 0)]
CROSS = [("q", 0, 128, 0, 0), ("q", 128, 256, 1, 0), ("s", 0, 256, 1, 0), ("q", 256, 512, 2, 1), ("s", 256, 512, 2, 1)]
SECOND = [("q", 0, 512, "s", 0), ("s", 0, 512, "s", 0)]
GROUPS = [(0, 256), (256, 512)]
ROUTE = [(0, [("q", 0, 128, 0, 0)]), (1, [("q", 128, 256, 0, 1)]), (1, [("s", 0, 256, 0, 2)]),
         (2, [("q", 256, 384, 1, 0), ("q", 384, 512, 1, 1)]), (2, [("s", 256, 512, 1, 2)])]


def pick(mask, n, skip=0):
    bits = [b for b in range(16) if (mask >> b) & 1 and not (skip >> b) & 1]
    return sum(1 << b for b in bits[::len(bits) // n][:n])


def count(mask):
    return sum((mask >> b) & 1 for b in range(16))


def relays(T, topo, r):
    src, dst = T.cores[r], T.cores[(r - 1) % RANKS]
    if topo.may_write(src, dst):
        return None
    sc, dc = topo.chip(src), topo.chip(dst)
    free = [c for c in range(8 * RANKS) if T.rank_of(c) is None and topo.may_write(c, dst)]
    near = [c for c in free if topo.chip(c) == sc and topo.die(c) == topo.die(src)]
    far = [c for c in free if topo.mates(topo.chip(c), dc) and topo.same_plane(topo.chip(c), sc)]
    same = [c for c in far if topo.die(c) == topo.die(src)]
    other = [c for c in far if topo.die(c) != topo.die(src)]
    return near[0], same[0], other[0]


def k_first(T, topo, r):
    return relays(T, topo, r) is not None or relays(T, topo, (r - 1) % RANKS) is not None


def first_hops(T, topo, r):
    rel, src, out, k = relays(T, topo, r), T.cores[r], [], 0
    mb = pick(topo.mask(src, rel[1]), RB)
    ma = pick(topo.mask(src, rel[0]), RA, mb)
    for ch, tr in ROUTE:
        c = []
        for kind, lo, hi, gr, j in tr:
            c.append((kind, lo, hi, gr, rel[j], mb if j else ma, "f%d" % k))
            k += 1
        out.append((ch, c))
    return out


def side(q, s, kind, lo, hi):
    return q[:, lo:hi].bitcast(dt.uint8) if kind == "q" else s[:, lo:hi]


def relay_core(g, core, T, topo):
    n = 0
    for r in range(RANKS):
        if relays(T, topo, r) is None:
            continue
        dst = T.cores[(r - 1) % RANKS]
        rid, pid, _ = topo.addr(dst)
        for _, tr in first_hops(T, topo, r):
            for kind, lo, hi, gr, c, m1, f in tr:
                if c == core:
                    m = pick(topo.mask(core, dst), ROFF)
                    g.wait_ge(T.sem[f], count(m1))
                    g.remote_dma(side(T.rqk, T.rsk, kind, lo, hi), side(T.qk, T.sk, kind, lo, hi),
                                 T.sem["ak%d" % gr], T.sem.sent, pid, rid, m)
                    n += count(m)
    if n:
        g.wait_ge(T.sem.sent, n)


def rank_program(g, core, T, topo):
    rank = T.rank_of(core)
    if rank is None:
        return relay_core(g, core, T, topo)
    S, V, A, E, Y = T.sem, g.vector, g.scalar, g.tensor, g.sync
    nxt, prv = (rank + 1) % RANKS, (rank - 1) % RANKS
    chip = [topo.chip(c) for c in T.cores]
    kfirst = k_first(T, topo, rank)
    last = len(CHUNKS) - 1

    if kfirst:
        (ina, ta, qa, sa), (inb, tb, qb, sb) = (T.x, T.xt, T.qx, T.sx), (T.w1, T.wt, T.qw, T.sw)
        (pt, qp, sp), (st, qs, ss) = (T.kt, T.qk, T.sk), (T.ht, T.qh, T.sh)
    else:
        (ina, ta, qa, sa), (inb, tb, qb, sb) = (T.w1, T.wt, T.qw, T.sw), (T.x, T.xt, T.qx, T.sx)
        (pt, qp, sp), (st, qs, ss) = (T.ht, T.qh, T.sh), (T.kt, T.qk, T.sk)
    Y.dma_start(ta[:, 0:1024], ina[:, 0:1024]).then_inc(S.la0, 16)
    A.dma_start(ta[:, 1024:2048], ina[:, 1024:2048]).then_inc(S.la1, 16)
    for c, (lo, hi) in enumerate(CHUNKS):
        (A if c % 2 else Y).dma_start(tb[:, 4 * lo:4 * hi], inb[:, 4 * lo:4 * hi]).then_inc(S["lb%d" % c], 16)
    Y.dma_start(T.et[:], T.e[:]).then_inc(S.le, 16)
    A.dma_start(T.vt[:], T.w2[:]).then_inc(S.lv, 16)

    ps = [(T.pa, T.pb)[c % 2] for c in range(last + 2)]
    E.wait_ge(S.va, 2)
    for c, (lo, hi) in enumerate(CHUNKS):
        E.wait_ge(S["vb%d" % c], 1)
        if c >= 2:
            E.wait_ge(S["ap%d" % (c - 2)], 4)
        for i in range(4):
            E.matmul_mx(ps[c][:, 512 * i:512 * i + hi - lo], qa[:, 128 * i:128 * i + 128], sa[:, 128 * i:128 * i + 128],
                        qb[:, lo:hi], sb[:, lo:hi], True, True).then_inc(S["m%d" % (4 * c + i)], 1)
    E.wait_ge(S["ap%d" % (last - 1)], 4)
    for i in range(4):
        E.matmul_mx(ps[last + 1][:, 512 * i:512 * i + 512], qb[:, 128 * i:128 * i + 128], sb[:, 128 * i:128 * i + 128],
                    qa[:], sa[:], True, True).then_inc(S["n%d" % i], 1)

    def quant(q, s, t, lo, hi):
        return V.quantize_mx(q[:, lo:hi], s[:, lo:hi], t[:, 4 * lo:4 * hi])

    def steps(onvec, ready, out, in_):
        if onvec:
            V.wait_ge(ready, 1)
            return V.tensor_scalar(out, in_, 0.0, COEF, AluOpType.max, AluOpType.mult)
        A.wait_ge(ready, 1)
        return A.activation(out, in_, ActivationFunctionType.Relu, scale=COEF)

    for u in range(2):
        V.wait_ge(S["la%d" % u], 16)
        quant(qa, sa, ta, 256 * u, 256 * u + 256).then_inc(S.va, 1)
    for what in ORDER:
        c = int(what[1])
        lo, hi = CHUNKS[c]
        if what[0] == "b":
            V.wait_ge(S["lb%d" % c], 16)
            quant(qb, sb, tb, lo, hi).then_inc(S["vb%d" % c], 1)
            continue
        for i in range(4):
            steps(i in VFIRST, S["m%d" % (4 * c + i)], pt[:, 4 * lo + i:4 * hi:4],
                  ps[c][:, 512 * i:512 * i + hi - lo]).then_inc(S["ap%d" % c], 1)
        V.wait_ge(S["ap%d" % c], 4)
        quant(qp, sp, pt, lo, hi).then_inc(S["vp%d" % c], 1)
    V.wait_ge(S.le, 16)
    quant(T.qe, T.se, T.et, 0, 256).then_inc(S.ve, 1)
    V.wait_ge(S.lv, 16)
    quant(T.qv, T.sv, T.vt, 0, 128).then_inc(S.vv, 1)
    for i in range(4):
        steps(i in VSECOND, S["n%d" % i], st[:, i:2048:4], ps[last + 1][:, 512 * i:512 * i + 512]).then_inc(S["as"], 1)
    V.wait_ge(S["as"], 4)
    quant(qs, ss, st, 0, 512).then_inc(S.vs, 1)

    bufs = {"h": (T.qh, T.sh, T.rqh, T.rsh), "k": (T.qk, T.sk, T.rqk, T.rsk)}
    sent, seen = [0], {}

    def writes(frm, which):
        if (which == "k") != k_first(T, topo, frm):
            return SECOND
        to = (frm + 1) % RANKS if which == "h" else (frm - 1) % RANKS
        return WHOLE if chip[to] == chip[frm] else CROSS

    def ready(ch):
        for c in list(range(last + 1 if ch == "s" else ch + 1)) + (["s"] if ch == "s" else []):
            if c not in seen:
                g.wait_ge(S["vs" if c == "s" else "vp%d" % c], 1)
                seen[c] = True

    def send(which):
        q, s, rq, rs = bufs[which]
        to = nxt if which == "h" else prv
        rid, pid, _ = topo.addr(T.cores[to])
        m = pick(topo.mask(core, T.cores[to]), ON if chip[to] == chip[rank] else OFF)
        for kind, lo, hi, ch, gr in writes(rank, which):
            ready(ch)
            g.remote_dma(side(rq, rs, kind, lo, hi), side(q, s, kind, lo, hi), S["a%s%d" % (which, gr)], S.sent, pid, rid, m)
            sent[0] += count(m)

    if relays(T, topo, rank) is None:
        send("k" if kfirst else "h")
    else:
        for ch, tr in first_hops(T, topo, rank):
            ready(ch)
            parts = []
            for kind, lo, hi, gr, c, m, f in tr:
                rid, pid, _ = topo.addr(c)
                parts.append(RemoteDMATransfer(dst_ids=[DstId(rid=rid, pnc=pid)], dma_engine_mask=m, remote_sem=S[f],
                                               srcs=[side(T.qk, T.sk, kind, lo, hi)], dsts=[side(T.qk, T.sk, kind, lo, hi)]))
                sent[0] += count(m)
            g.remote_dma_fused(parts, local_sem=S.sent)
    send("h" if kfirst else "k")
    g.wait_ge(S.sent, sent[0])

    def arriving(which):
        frm = prv if which == "h" else nxt
        inc = [0, 0]
        if which == "k" and relays(T, topo, frm) is not None:
            for _, tr in first_hops(T, topo, frm):
                for t in tr:
                    inc[t[3]] += ROFF
        else:
            for w in writes(frm, which):
                inc[w[4]] += ON if chip[frm] == chip[rank] else OFF
        if not inc[1]:
            return [("a%s0" % which, inc[0], 0, 512)]
        return [("a%s%d" % (which, u), inc[u], *GROUPS[u]) for u in range(2)]

    def copy(onvec, ready_, out, in_):
        if onvec:
            V.wait_ge(ready_, 1)
            return V.tensor_copy(out, in_)
        A.wait_ge(ready_, 1)
        return A.activation(out, in_, ActivationFunctionType.Copy)

    def second_y():
        E.wait_ge(S.vv, 1)
        for sem, inc, lo, hi in arriving("h"):
            E.wait_ge(S[sem], inc)
            for u in range(lo // 256, hi // 256):
                a, b = 256 * u, 256 * u + 256
                E.matmul_mx(T.pa[:, 512 * u:512 * u + 256], T.qv[:], T.sv[:], T.rqh[:, a:b], T.rsh[:, a:b],
                            True, True).then_inc(S["my%d" % u], 1)
                copy(u == 1, S["my%d" % u], T.yo[:, a:b], T.pa[:, 512 * u:512 * u + 256]).then_inc(S["cy%d" % u], 1)
                Y.wait_ge(S["cy%d" % u], 1)
            Y.dma_start(T.y[:, lo:hi], T.yo[:, lo:hi]).then_inc(S.sty, 16)

    def second_z():
        E.wait_ge(S.ve, 1)
        for sem, inc, lo, hi in arriving("k"):
            E.wait_ge(S[sem], inc)
            for b in range(lo // 128, hi // 128):
                E.matmul_mx(T.pb[:, 512 * b:512 * b + 256], T.rqk[:, 128 * b:128 * b + 128], T.rsk[:, 128 * b:128 * b + 128],
                            T.qe[:], T.se[:], True, True).then_inc(S["mz%d" % b], 1)
                copy(b % 2 == 1, S["mz%d" % b], T.zo[:, 256 * b:256 * b + 256],
                     T.pb[:, 512 * b:512 * b + 256]).then_inc(S["cz%d" % b], 1)
                Y.wait_ge(S["cz%d" % b], 1)
            Y.dma_start(T.z[:, 2 * lo:2 * hi], T.zo[:, 2 * lo:2 * hi]).then_inc(S.stz, 16)

    E.wait_ge(S["as"], 4)
    E.wait_ge(S["ap%d" % last], 4)
    if kfirst:
        second_z()
        second_y()
    else:
        second_y()
        second_z()
    Y.wait_ge(S.sty, 16 * len(arriving("h")))
    Y.wait_ge(S.stz, 16 * len(arriving("k")))
